import numpy as np
import ml_dtypes


def mxq(x, axis, fmt="e4m3"):
    dtype, down = {"e4m3": (ml_dtypes.float8_e4m3fn, 7), "e5m2": (ml_dtypes.float8_e5m2, 14)}[fmt]
    v = np.moveaxis(np.asarray(x, np.float32).astype(ml_dtypes.bfloat16).astype(np.float64), axis, -1)
    blocks = v.reshape(v.shape[:-1] + (-1, 32))
    amax = np.abs(blocks).max(-1, keepdims=True)
    byte = np.maximum(np.where(amax > 0, np.frexp(amax)[1] - 1 + 127, 0) - down, 1)
    scale = np.exp2(byte - 127.0)
    codes = (blocks / scale).astype(np.float32).astype(dtype).astype(np.float64)
    return np.moveaxis((codes * scale).reshape(v.shape), -1, axis)


WIDE = False


def mx_kscale(k):
    if not WIDE:
        return np.ones(k)
    levels = np.array([10, -10, 5, -5, 0])
    if k % 512:
        return np.exp2(np.random.permutation(np.resize(levels, k // 32))).repeat(32)
    a = np.empty((k // 512, 16))
    for p in range(k // 512):
        a[p, :8] = np.random.permutation(np.resize(levels, 8))
        for g in range(8):
            far = levels[np.abs(levels - a[p, g]) >= 10]
            a[p, g + 8] = far[np.random.randint(len(far))]
    return np.exp2(a.ravel()).repeat(32)


def f64(x):
    return np.asarray(x).astype(np.float64)


def striped(idx):
    return np.tile(np.asarray(idx).reshape(-1, 16).T, (8, 1)).astype(np.uint16)


def unstriped(offs):
    return offs[:16].T.reshape(-1).astype(np.int64)


E2M1 = np.array([0.0, 0.5, 1.0, 1.5, 2.0, 3.0, 4.0, 6.0, -0.0, -0.5, -1.0, -1.5, -2.0, -3.0, -4.0, -6.0])


def pack_weight(w, fmt):
    k, n = w.shape
    w = f64(np.asarray(w, np.float32).astype(ml_dtypes.bfloat16)).reshape(k // 32, 32, n)
    amax = np.abs(w).max(1)
    if fmt == "e4m3":
        byte = np.frexp(amax)[1] - 1 + 127 - 7
    else:
        mant, ex = np.frexp(amax / 6.0)
        byte = np.where(mant > 0.5, ex, ex - 1) + 127
    byte = np.clip(np.where(amax > 0, byte, 1), 1, 254)
    scaled = (w * np.exp2(127.0 - byte)[:, None, :]).reshape(k, n).astype(np.float32)
    by_word = np.ascontiguousarray(scaled.reshape(k // 512, 128, 4, n).transpose(0, 1, 3, 2))
    if fmt == "e4m3":
        words = by_word.astype(ml_dtypes.float8_e4m3fn).view(np.uint8)
    else:
        c = by_word.astype(ml_dtypes.float4_e2m1fn).view(np.uint8) & 0xF
        words = (c[..., 0::2] | (c[..., 1::2] << 4)).reshape(k // 512, 128, 2 * n)
    return np.ascontiguousarray(words), np.ascontiguousarray(byte.astype(np.uint8).reshape(k // 512, 16, n))


def unpack_weight(words, scales, fmt):
    g, _, n = scales.shape
    words = np.ascontiguousarray(words).reshape(g, 128, n, -1)
    if fmt == "e4m3":
        vals = words.view(ml_dtypes.float8_e4m3fn).astype(np.float64)
    else:
        nib = np.empty((g, 128, n, 4), np.uint8)
        nib[..., 0::2] = words & 0xF
        nib[..., 1::2] = words >> 4
        vals = E2M1[nib]
    vals = vals * np.repeat(np.exp2(scales.astype(np.float64) - 127.0), 8, axis=1)[..., None]
    return vals.transpose(0, 1, 3, 2).reshape(g * 512, n)


def bf(x):
    return np.asarray(x, np.float32).astype(ml_dtypes.bfloat16)


def planes(Y):
    r, m = Y.shape
    b = f64(bf(Y)).reshape(r // 32, 32, m)
    amax = np.abs(b).max(1)
    byte = np.clip(np.where(amax > 0, np.frexp(amax)[1] - 1 + 127 - 7, 1), 1, 254)
    codes = (b * np.exp2(127.0 - byte)[:, None, :]).reshape(r, m).astype(np.float32).astype(ml_dtypes.float8_e4m3fn).view(np.uint8)
    words = codes.reshape(r // 512, 128, 4, m).transpose(0, 1, 3, 2)
    return np.ascontiguousarray(words), np.ascontiguousarray(byte.astype(np.uint8).reshape(r // 512, 16, m))


D, T, I, Q, G = 512, 2048, 512, 1024, 64


def setup_inputs():
    n = np.random.standard_normal
    idx = np.random.permutation(T)[:I]
    fd = mx_kscale(D)
    keysp = pack_weight(n((D, T)) / fd[:, None], "e2m1")
    return {
        "query": (n((D, Q)) * 0.4 / np.sqrt(D) * fd[:, None]).astype(np.float32),
        "keys_words": keysp[0],
        "keys_scales": keysp[1],
        "offs": striped(idx),
    }


def reference(query, keys_words, keys_scales, offs):
    idx = unstriped(offs)
    keysu = unpack_weight(keys_words, keys_scales, "e2m1")
    queryq = mxq(f64(query), 0, "e4m3")
    keysidxg = keysu[:, idx]
    a = queryq.T @ keysidxg
    p = np.exp(a - np.max(a, axis=1, keepdims=True))
    w = p / np.sum(p, axis=1, keepdims=True)
    w1 = np.pad(w, ((0, 0), (1, 0)))[:, :I]
    w2 = np.pad(w, ((0, 0), (2, 0)))[:, :I]
    w3 = np.pad(w, ((0, 0), (3, 0)))[:, :I]
    w4 = np.pad(w, ((0, 0), (4, 0)))[:, :I]
    s = (w + w1 + w2 + w3 + w4) * 102.4
    st = s.T
    y = st.reshape(I, G, Q // G).sum(axis=2)
    words, scales = planes(y)
    return y, words, scales

@@ -1,0 +1,191 @@
+from contextlib import ExitStack
+
+import concourse.mybir as mybir
+from concourse.masks import make_identity
+
+D, T, I, Q, G = 512, 2048, 512, 1024, 64
+FLOPS = 2 * D * I * Q
+
+F32 = mybir.dt.float32
+BF16 = mybir.dt.bfloat16
+I32 = mybir.dt.int32
+U32 = mybir.dt.uint32
+U16 = mybir.dt.uint16
+U8 = mybir.dt.uint8
+FP8X4 = mybir.dt.float8_e4m3fn_x4
+FP4X4 = mybir.dt.float4_e2m1fn_x4
+ALU = mybir.AluOpType
+ACT = mybir.ActivationFunctionType
+AXIS = mybir.AxisListType
+
+P = 128
+PACK = 4
+ROWS = Q // G
+GROUPS = 2
+HG = G // GROUPS
+H = P // HG
+TILES = ROWS // H
+BLOCKS = PACK // H
+SPILL = H - 1
+CHUNKS = [[0,16,[["s",0,16]]],[16,32,[["s",16,24],["v",24,32]]],[32,48,[["s",32,48]]],[48,64,[["s",48,56],["v",56,64]]]]
+SCALE_ENG = "ggggggvv"
+
+
+def tile_attend_votes_pl_kernel(tc, query, keys_words, keys_scales, offs, out_0, out_1, out_2):
+    nc = tc.nc
+    with ExitStack() as ctx:
+        keep = ctx.enter_context(tc.tile_pool(name="keep", bufs=1))
+        ring = ctx.enter_context(tc.tile_pool(name="ring", bufs=3))
+        psum = ctx.enter_context(tc.psum_pool(name="psum", bufs=1))
+        pscore = ctx.enter_context(tc.psum_pool(name="pscore", bufs=4))
+
+        offsets = keep.tile([P, I // 16], U16, name="offsets")
+        nc.sync.dma_start(offsets[:], offs)
+        pool_words = keep.tile([P, T], U16, name="pool_words", align_bytes=64)
+        nc.sync.dma_start(pool_words[:].bitcast(I32), keys_words[0].bitcast(I32))
+        pool_scales = keep.tile([P, T], U8, name="pool_scales", align_bytes=64)
+        nc.vector.memset(pool_scales[:].bitcast(I32), 0)
+        for quad in range(4):
+            nc.sync.dma_start(
+                pool_scales[32 * quad : 32 * quad + 4, :].bitcast(I32),
+                keys_scales[0, 4 * quad : 4 * quad + 4, :].bitcast(I32),
+            )
+        query_rows = query.rearrange("(p d) q -> p d q", d=PACK)
+        raws = []
+        for c, (g0, g1, parts) in enumerate(CHUNKS):
+            raw = keep.tile([P, PACK, (g1 - g0) * ROWS], F32, name=f"raw{c}")
+            nc.sync.dma_start(raw[:], query_rows[:, :, g0 * ROWS : g1 * ROWS])
+            raws.append(raw)
+
+        warm = keep.tile([P, 2], F32, name="warm")
+        nc.vector.memset(warm[:, 0:1], 0.0)
+        nc.scalar.activation(warm[:, 1:2], warm[:, 0:1], ACT.Exp)
+
+        ident = keep.tile([P, P], F32, name="ident")
+        make_identity(nc, ident[:])
+
+        key_words = keep.tile([P, I], U16, name="key_words", align_bytes=64)
+        key_scales = keep.tile([P, I], U8, name="key_scales", align_bytes=64)
+        nc.vector.tensor_copy(key_words[:], pool_words[:].indirect(offsets[:]))
+        nc.vector.tensor_copy(key_scales[:], pool_scales[:].indirect(offsets[:]))
+
+        grouped = [
+            keep.tile([P, TILES, HG, H, PACK], BF16, name=f"grouped{a}", align_bytes=64)
+            for a in range(GROUPS)
+        ]
+        for c, (g0, g1, parts) in enumerate(CHUNKS):
+            for eng, e0, e1 in parts:
+                a = e0 // HG
+                src = raws[c][:, :, (e0 - g0) * ROWS : (e1 - g0) * ROWS]
+                dst = grouped[a][:, :, e0 - a * HG : e1 - a * HG, :, :]
+                if eng == "g":
+                    nc.gpsimd.tensor_scalar(
+                        dst.rearrange("p t g h d -> p g t h d"),
+                        src.rearrange("p d (g t h) -> p g t h d", t=TILES, h=H),
+                        1.0, 0.0, ALU.mult, ALU.add,
+                    )
+                else:
+                    copy = nc.vector.tensor_copy if eng == "v" else nc.scalar.copy
+                    copy(
+                        dst.rearrange("p t g h d -> p g t d h"),
+                        src.rearrange("p d (g t h) -> p g t d h", t=TILES, h=H),
+                    )
+
+        y = keep.tile([P, PACK, G], F32, name="y")
+        y_bf = keep.tile([P, G, PACK], BF16, name="y_bf", align_bytes=64)
+
+        for a in range(GROUPS):
+            smooth = psum.tile([P, PACK + SPILL + 1 + H, HG], F32, name=f"smooth{a}")
+            nc.tensor.matmul(
+                smooth[:, PACK + SPILL + 1 : PACK + SPILL + 1 + H, :].rearrange("p j g -> p (j g)"),
+                lhsT=ident[:], rhs=ident[:], start=True, stop=False, is_transpose=True,
+            )
+            votes = psum.tile([P, PACK, P], F32, name=f"votes{a}", tag=f"votes{a}")
+            for t in range(TILES):
+                n = a * TILES + t
+                q_codes = keep.tile([P, P], U32, name=f"q_codes{n}", align_bytes=64)
+                q_scales = keep.tile([P, P], U8, name=f"q_scales{n}", align_bytes=64)
+                nc.vector.quantize_mx(
+                    out=q_codes[:].bitcast(FP8X4),
+                    scales=q_scales[:],
+                    in_=grouped[a][:, t, :, :, :].rearrange("p g h d -> p (g h d)"),
+                )
+                scores = pscore.tile([P, I], F32, name="scores")
+                nc.tensor.matmul_mx(
+                    out=scores[:],
+                    lhsT=q_codes[:].bitcast(FP8X4),
+                    lhsT_scale=q_scales[:],
+                    rhs=key_words[:].bitcast(FP4X4),
+                    rhs_scale=key_scales[:],
+                    start=True,
+                    stop=True,
+                )
+                neg_max = keep.tile([P, 1], F32, name=f"neg_max{n}")
+                nc.vector.tensor_reduce(neg_max[:], scores[:], AXIS.X, ALU.max, negate=True)
+                probs = ring.tile([P, PACK, P], F32, name="probs")
+                row_sum = keep.tile([P, 1], F32, name=f"row_sum{n}")
+                nc.scalar.activation(
+                    probs[:], scores[:].rearrange("p (s r) -> p r s", r=PACK), ACT.Exp,
+                    bias=neg_max[:], accum_out=row_sum[:],
+                )
+                inv_sum = keep.tile([P, 1], F32, name=f"inv_sum{n}")
+                nc.vector.reciprocal(inv_sum[:], row_sum[:])
+                weights = ring.tile([P, PACK, P], F32, name="weights")
+                eng = nc.vector if SCALE_ENG[n] == "v" else nc.gpsimd
+                eng.tensor_scalar(weights[:], probs[:], inv_sum[:], 102.4, ALU.mult, ALU.mult)
+                for r in range(PACK):
+                    nc.tensor.matmul(
+                        votes[:, r, :], lhsT=weights[:, r, :], rhs=ident[:],
+                        start=(t == 0 and r == 0), stop=(t == TILES - 1 and r == PACK - 1),
+                        is_transpose=True,
+                    )
+            by_slot = keep.tile([P, PACK, HG], F32, name=f"by_slot{a}")
+            nc.vector.tensor_reduce(
+                by_slot[:], votes[:].rearrange("p r (g h) -> p r g h", h=H), AXIS.X, ALU.add
+            )
+            back = psum.tile([P, BLOCKS, P], F32, name=f"back{a}", tag=f"votes{a}")
+            for b in range(BLOCKS):
+                nc.tensor.transpose(
+                    back[:, b, :],
+                    by_slot[:, b * H : (b + 1) * H, :].rearrange("p r g -> p (r g)"),
+                    ident[:],
+                )
+            padded = keep.tile([P, BLOCKS, P + 8], F32, name=f"padded{a}")
+            nc.gpsimd.memset(padded[:, :, 0:8], 0.0)
+            nc.scalar.copy(padded[:, :, 8:], back[:])
+            steps = []
+            for b in range(BLOCKS):
+                for k in range(PACK - b * H):
+                    steps.append((b, 8, b * H + k))
+                for k in range(b * H + H):
+                    steps.append((b, 7, b * H - k))
+            first = [-SPILL + H * m for m in range((PACK + SPILL + 1) // H)]
+            lead = []
+            for j in first:
+                lead.append([s for s in steps if s[2] == j][0])
+            steps = lead + [s for s in steps if s not in lead]
+            for m, (b, c0, j) in enumerate(steps):
+                nc.tensor.matmul(
+                    smooth[:, SPILL + j : SPILL + j + H, :].rearrange("p j g -> p (j g)"),
+                    lhsT=padded[:, b, c0 : c0 + P], rhs=ident[:],
+                    start=False, stop=(m == len(steps) - 1), is_transpose=True,
+                )
+            heads = slice(a * HG, (a + 1) * HG)
+            result = smooth[:, SPILL : SPILL + PACK, :]
+            nc.vector.tensor_copy(y_bf[:, heads, :], result.rearrange("p r g -> p g r"))
+            nc.scalar.copy(y[:, :, heads], result)
+
+        nc.sync.dma_start(out_0.rearrange("(s r) g -> s r g", r=PACK), y[:])
+        y_codes = keep.tile([P, G], U32, name="y_codes", align_bytes=64)
+        y_scales = keep.tile([P, G], U8, name="y_scales", align_bytes=64)
+        nc.vector.quantize_mx(
+            out=y_codes[:].bitcast(FP8X4), scales=y_scales[:],
+            in_=y_bf[:].rearrange("p g r -> p (g r)"),
+        )
+        nc.sync.dma_start(out_1[0].rearrange("p c r -> p (c r)").bitcast(I32), y_codes[:].bitcast(I32))
+        for quad in range(4):
+            queue = nc.scalar if quad % 2 == 0 else nc.sync
+            queue.dma_start(
+                out_2[0, 4 * quad : 4 * quad + 4, :].bitcast(I32),
+                y_scales[32 * quad : 32 * quad + 4, :].bitcast(I32),
+            )

@@ -27,17 +27,18 @@ H = P // HG
 TILES = ROWS // H
 BLOCKS = PACK // H
 SPILL = H - 1
-CHUNKS = [[0,16,[["s",0,16]]],[16,32,[["s",16,24],["v",24,32]]],[32,48,[["s",32,48]]],[48,64,[["s",48,56],["v",56,64]]]]
-SCALE_ENG = "ggggggvv"
+CHUNKS = [[0,16,[["s",0,16]]],[16,32,[["s",16,22],["v",22,32]]],[32,48,[["s",32,48]]],[48,64,[["s",48,64]]]]
+QUANT = {0: 1, 1: 1, 2: 2, 4: 4}
+BATCHES = [[0,1],[2,3],[4,5],[6],[7]]
+SCALE_ENG = "vsvsvsvv"
 
 
 def tile_attend_votes_pl_kernel(tc, query, keys_words, keys_scales, offs, out_0, out_1, out_2):
     nc = tc.nc
     with ExitStack() as ctx:
         keep = ctx.enter_context(tc.tile_pool(name="keep", bufs=1))
-        ring = ctx.enter_context(tc.tile_pool(name="ring", bufs=3))
         psum = ctx.enter_context(tc.psum_pool(name="psum", bufs=1))
-        pscore = ctx.enter_context(tc.psum_pool(name="pscore", bufs=4))
+        pscore = ctx.enter_context(tc.psum_pool(name="pscore", bufs=6))
 
         offsets = keep.tile([P, I // 16], U16, name="offsets")
         nc.sync.dma_start(offsets[:], offs)
@@ -87,34 +88,33 @@ def tile_attend_votes_pl_kernel(tc, query, keys_words, keys_scales, offs, out_0,
                 else:
                     copy = nc.vector.tensor_copy if eng == "v" else nc.scalar.copy
                     copy(
-                        dst.rearrange("p t g h d -> p g t d h"),
-                        src.rearrange("p d (g t h) -> p g t d h", t=TILES, h=H),
+                        dst.rearrange("p t g h d -> p g t h d"),
+                        src.rearrange("p d (g t h) -> p g t h d", t=TILES, h=H),
                     )
 
         y = keep.tile([P, PACK, G], F32, name="y")
         y_bf = keep.tile([P, G, PACK], BF16, name="y_bf", align_bytes=64)
 
+        q_codes = [keep.tile([P, TILES * P], U32, name=f"q_codes{a}", align_bytes=64) for a in range(GROUPS)]
+        q_scales = [keep.tile([P, TILES * P], U8, name=f"q_scales{a}", align_bytes=64) for a in range(GROUPS)]
+        votes = [psum.tile([P, PACK, P], F32, name=f"votes{a}", tag=f"votes{a}") for a in range(GROUPS)]
+        probs = []
         for a in range(GROUPS):
-            smooth = psum.tile([P, PACK + SPILL + 1 + H, HG], F32, name=f"smooth{a}")
-            nc.tensor.matmul(
-                smooth[:, PACK + SPILL + 1 : PACK + SPILL + 1 + H, :].rearrange("p j g -> p (j g)"),
-                lhsT=ident[:], rhs=ident[:], start=True, stop=False, is_transpose=True,
-            )
-            votes = psum.tile([P, PACK, P], F32, name=f"votes{a}", tag=f"votes{a}")
             for t in range(TILES):
                 n = a * TILES + t
-                q_codes = keep.tile([P, P], U32, name=f"q_codes{n}", align_bytes=64)
-                q_scales = keep.tile([P, P], U8, name=f"q_scales{n}", align_bytes=64)
-                nc.vector.quantize_mx(
-                    out=q_codes[:].bitcast(FP8X4),
-                    scales=q_scales[:],
-                    in_=grouped[a][:, t, :, :, :].rearrange("p g h d -> p (g h d)"),
-                )
-                scores = pscore.tile([P, I], F32, name="scores")
+                if n in QUANT:
+                    cols = slice(t * P, (t + QUANT[n]) * P)
+                    nc.vector.quantize_mx(
+                        out=q_codes[a][:, cols].bitcast(FP8X4),
+                        scales=q_scales[a][:, cols],
+                        in_=grouped[a][:, t : t + QUANT[n], :, :, :].rearrange("p t g h d -> p (t g h d)"),
+                    )
+                cols = slice(t * P, (t + 1) * P)
+                scores = pscore.tile([P, I], F32, name="scores", tag="bank")
                 nc.tensor.matmul_mx(
                     out=scores[:],
-                    lhsT=q_codes[:].bitcast(FP8X4),
-                    lhsT_scale=q_scales[:],
+                    lhsT=q_codes[a][:, cols].bitcast(FP8X4),
+                    lhsT_scale=q_scales[a][:, cols],
                     rhs=key_words[:].bitcast(FP4X4),
                     rhs_scale=key_scales[:],
                     start=True,
@@ -122,60 +122,70 @@ def tile_attend_votes_pl_kernel(tc, query, keys_words, keys_scales, offs, out_0,
                 )
                 neg_max = keep.tile([P, 1], F32, name=f"neg_max{n}")
                 nc.vector.tensor_reduce(neg_max[:], scores[:], AXIS.X, ALU.max, negate=True)
-                probs = ring.tile([P, PACK, P], F32, name="probs")
-                row_sum = keep.tile([P, 1], F32, name=f"row_sum{n}")
+                probs.append(keep.tile([P, PACK, P], F32, name=f"probs{n}"))
+                batch = [bt for bt in BATCHES if n in bt][0]
+                if n == batch[0]:
+                    row_sum = keep.tile([P, len(batch)], F32, name=f"row_sum{n}")
+                place = n - batch[0]
                 nc.scalar.activation(
-                    probs[:], scores[:].rearrange("p (s r) -> p r s", r=PACK), ACT.Exp,
-                    bias=neg_max[:], accum_out=row_sum[:],
+                    probs[n][:], scores[:].rearrange("p (s r) -> p r s", r=PACK), ACT.Exp,
+                    bias=neg_max[:], accum_out=row_sum[:, place : place + 1],
                 )
-                inv_sum = keep.tile([P, 1], F32, name=f"inv_sum{n}")
+                if n != batch[-1]:
+                    continue
+                inv_sum = keep.tile([P, len(batch)], F32, name=f"inv_sum{n}")
                 nc.vector.reciprocal(inv_sum[:], row_sum[:])
-                weights = ring.tile([P, PACK, P], F32, name="weights")
-                eng = nc.vector if SCALE_ENG[n] == "v" else nc.gpsimd
-                eng.tensor_scalar(weights[:], probs[:], inv_sum[:], 102.4, ALU.mult, ALU.mult)
-                for r in range(PACK):
-                    nc.tensor.matmul(
-                        votes[:, r, :], lhsT=weights[:, r, :], rhs=ident[:],
-                        start=(t == 0 and r == 0), stop=(t == TILES - 1 and r == PACK - 1),
-                        is_transpose=True,
-                    )
-            by_slot = keep.tile([P, PACK, HG], F32, name=f"by_slot{a}")
-            nc.vector.tensor_reduce(
-                by_slot[:], votes[:].rearrange("p r (g h) -> p r g h", h=H), AXIS.X, ALU.add
-            )
-            back = psum.tile([P, BLOCKS, P], F32, name=f"back{a}", tag=f"votes{a}")
-            for b in range(BLOCKS):
-                nc.tensor.transpose(
-                    back[:, b, :],
-                    by_slot[:, b * H : (b + 1) * H, :].rearrange("p r g -> p (r g)"),
-                    ident[:],
-                )
-            padded = keep.tile([P, BLOCKS, P + 8], F32, name=f"padded{a}")
-            nc.gpsimd.memset(padded[:, :, 0:8], 0.0)
-            nc.scalar.copy(padded[:, :, 8:], back[:])
-            steps = []
-            for b in range(BLOCKS):
-                for k in range(PACK - b * H):
-                    steps.append((b, 8, b * H + k))
-                for k in range(b * H + H):
-                    steps.append((b, 7, b * H - k))
-            first = [-SPILL + H * m for m in range((PACK + SPILL + 1) // H)]
-            lead = []
-            for j in first:
-                lead.append([s for s in steps if s[2] == j][0])
-            steps = lead + [s for s in steps if s not in lead]
-            for m, (b, c0, j) in enumerate(steps):
-                nc.tensor.matmul(
-                    smooth[:, SPILL + j : SPILL + j + H, :].rearrange("p j g -> p (j g)"),
-                    lhsT=padded[:, b, c0 : c0 + P], rhs=ident[:],
-                    start=False, stop=(m == len(steps) - 1), is_transpose=True,
-                )
-            heads = slice(a * HG, (a + 1) * HG)
-            result = smooth[:, SPILL : SPILL + PACK, :]
-            nc.vector.tensor_copy(y_bf[:, heads, :], result.rearrange("p r g -> p g r"))
-            nc.scalar.copy(y[:, :, heads], result)
+                for m in batch:
+                    inv = inv_sum[:, m - batch[0] : m - batch[0] + 1]
+                    weights = keep.tile([P, PACK, P], F32, name=f"weights{m}")
+                    if SCALE_ENG[m] == "s":
+                        nc.scalar.activation(weights[:], probs[m][:], ACT.Copy, scale=inv)
+                    elif SCALE_ENG[m] == "v":
+                        nc.vector.tensor_scalar(weights[:], probs[m][:], inv, None, ALU.mult)
+                    else:
+                        nc.gpsimd.tensor_scalar(weights[:], probs[m][:], inv, 0.0, ALU.mult, ALU.add)
+                    for r in range(PACK):
+                        nc.tensor.matmul(
+                            votes[a][:, r, :], lhsT=weights[:, r, :], rhs=ident[:],
+                            start=(m % TILES == 0 and r == 0), stop=(m % TILES == TILES - 1 and r == PACK - 1),
+                            is_transpose=True,
+                        )
 
-        nc.sync.dma_start(out_0.rearrange("(s r) g -> s r g", r=PACK), y[:])
+        by_slot = keep.tile([P, PACK, G], F32, name="by_slot")
+        for a in range(GROUPS):
+            nc.vector.tensor_reduce(
+                by_slot[:, :, a * HG : (a + 1) * HG],
+                votes[a][:].rearrange("p r (g h) -> p r g h", h=H), AXIS.X, ALU.add,
+            )
+        back = pscore.tile([P, 2, P], F32, name="back", tag="bank")
+        for b in range(2):
+            nc.tensor.transpose(
+                back[:, b, :],
+                by_slot[:, 2 * b : 2 * b + 2, :].rearrange("p r g -> p (r g)"),
+                ident[:],
+            )
+        padded = keep.tile([P, 2, P + 8], F32, name="padded")
+        nc.gpsimd.memset(padded[:, :, 0:8], 0.0)
+        nc.scalar.activation(padded[:, :, 8:], back[:], ACT.Copy, scale=102.4)
+        smooth = pscore.tile([P, PACK + 2, G], F32, name="smooth", tag="bank")
+        steps = []
+        for b in range(2):
+            for k in range(PACK - 2 * b):
+                steps.append((b, 8, 2 * b + k))
+            for k in range(2 * b + 2):
+                steps.append((b, 7, 2 * b - k))
+        lead = [[s for s in steps if s[2] == j][0] for j in (-1, 1, 3)]
+        steps = lead + [s for s in steps if s not in lead]
+        for m, (b, c0, j) in enumerate(steps):
+            nc.tensor.matmul(
+                smooth[:, 1 + j : 3 + j, :].rearrange("p j g -> p (j g)"),
+                lhsT=padded[:, b, c0 : c0 + P], rhs=ident[:],
+                start=(m == 0), stop=(m == len(steps) - 1), is_transpose=True,
+            )
+        result = smooth[:, 1 : 1 + PACK, :]
+        nc.vector.tensor_copy(y_bf[:], result.rearrange("p r g -> p g r"))
+        nc.scalar.copy(y[:], result)
+
         y_codes = keep.tile([P, G], U32, name="y_codes", align_bytes=64)
         y_scales = keep.tile([P, G], U8, name="y_scales", align_bytes=64)
         nc.vector.quantize_mx(
@@ -183,8 +193,9 @@ def tile_attend_votes_pl_kernel(tc, query, keys_words, keys_scales, offs, out_0,
             in_=y_bf[:].rearrange("p g r -> p (g r)"),
         )
         nc.sync.dma_start(out_1[0].rearrange("p c r -> p (c r)").bitcast(I32), y_codes[:].bitcast(I32))
+        nc.scalar.dma_start(out_0.rearrange("(s r) g -> s r g", r=PACK), y[:])
         for quad in range(4):
-            queue = nc.scalar if quad % 2 == 0 else nc.sync
+            queue = nc.sync if quad < 2 else nc.scalar
             queue.dma_start(
                 out_2[0, 4 * quad : 4 * quad + 4, :].bitcast(I32),
                 y_scales[32 * quad : 32 * quad + 4, :].bitcast(I32),

@@ -27,10 +27,11 @@ H = P // HG
 TILES = ROWS // H
 BLOCKS = PACK // H
 SPILL = H - 1
-CHUNKS = [[0,16,[["s",0,16]]],[16,32,[["s",16,22],["v",22,32]]],[32,48,[["s",32,48]]],[48,64,[["s",48,64]]]]
+CHUNKS = [[0,16,[["s",0,16]]],[16,32,[["s",16,22],["v",22,32]]],[32,48,[["s",32,48]]],[48,64,[["s",48,54],["g",54,64]]]]
 QUANT = {0: 1, 1: 1, 2: 2, 4: 4}
-BATCHES = [[0,1],[2,3],[4,5],[6],[7]]
-SCALE_ENG = "vsvsvsvv"
+BATCHES = [[0,1],[2,3],[4,5,6],[7]]
+SCORE_BANKS = 4
+SCALE_ENG = "ggggvvvv"
 
 
 def tile_attend_votes_pl_kernel(tc, query, keys_words, keys_scales, offs, out_0, out_1, out_2):
@@ -38,7 +39,6 @@ def tile_attend_votes_pl_kernel(tc, query, keys_words, keys_scales, offs, out_0,
     with ExitStack() as ctx:
         keep = ctx.enter_context(tc.tile_pool(name="keep", bufs=1))
         psum = ctx.enter_context(tc.psum_pool(name="psum", bufs=1))
-        pscore = ctx.enter_context(tc.psum_pool(name="pscore", bufs=6))
 
         offsets = keep.tile([P, I // 16], U16, name="offsets")
         nc.sync.dma_start(offsets[:], offs)
@@ -97,7 +97,8 @@ def tile_attend_votes_pl_kernel(tc, query, keys_words, keys_scales, offs, out_0,
 
         q_codes = [keep.tile([P, TILES * P], U32, name=f"q_codes{a}", align_bytes=64) for a in range(GROUPS)]
         q_scales = [keep.tile([P, TILES * P], U8, name=f"q_scales{a}", align_bytes=64) for a in range(GROUPS)]
-        votes = [psum.tile([P, PACK, P], F32, name=f"votes{a}", tag=f"votes{a}") for a in range(GROUPS)]
+        early = psum.tile([P, PACK, P], F32, name="early")
+        late = [psum.tile([P, 2, P], F32, name=f"late{b}") for b in range(2)]
         probs = []
         for a in range(GROUPS):
             for t in range(TILES):
@@ -110,7 +111,7 @@ def tile_attend_votes_pl_kernel(tc, query, keys_words, keys_scales, offs, out_0,
                         in_=grouped[a][:, t : t + QUANT[n], :, :, :].rearrange("p t g h d -> p (t g h d)"),
                     )
                 cols = slice(t * P, (t + 1) * P)
-                scores = pscore.tile([P, I], F32, name="scores", tag="bank")
+                scores = psum.tile([P, I], F32, name="scores", tag=f"bank{n % SCORE_BANKS}")
                 nc.tensor.matmul_mx(
                     out=scores[:],
                     lhsT=q_codes[a][:, cols].bitcast(FP8X4),
@@ -141,33 +142,36 @@ def tile_attend_votes_pl_kernel(tc, query, keys_words, keys_scales, offs, out_0,
                     if SCALE_ENG[m] == "s":
                         nc.scalar.activation(weights[:], probs[m][:], ACT.Copy, scale=inv)
                     elif SCALE_ENG[m] == "v":
-                        nc.vector.tensor_scalar(weights[:], probs[m][:], inv, None, ALU.mult)
+                        cuts = (0, 2, 4) if m == GROUPS * TILES - 1 else (0, 4)
+                        for r0, r1 in zip(cuts, cuts[1:]):
+                            nc.vector.tensor_scalar(weights[:, r0:r1, :], probs[m][:, r0:r1, :], inv, None, ALU.mult)
                     else:
                         nc.gpsimd.tensor_scalar(weights[:], probs[m][:], inv, 0.0, ALU.mult, ALU.add)
+                    span = PACK if a == 0 else 2
                     for r in range(PACK):
                         nc.tensor.matmul(
-                            votes[a][:, r, :], lhsT=weights[:, r, :], rhs=ident[:],
-                            start=(m % TILES == 0 and r == 0), stop=(m % TILES == TILES - 1 and r == PACK - 1),
+                            early[:, r, :] if a == 0 else late[r // 2][:, r % 2, :], lhsT=weights[:, r, :], rhs=ident[:],
+                            start=(m % TILES == 0 and r % span == 0), stop=(m % TILES == TILES - 1 and r % span == span - 1),
                             is_transpose=True,
                         )
 
         by_slot = keep.tile([P, PACK, G], F32, name="by_slot")
-        for a in range(GROUPS):
-            nc.vector.tensor_reduce(
-                by_slot[:, :, a * HG : (a + 1) * HG],
-                votes[a][:].rearrange("p r (g h) -> p r g h", h=H), AXIS.X, ALU.add,
-            )
-        back = pscore.tile([P, 2, P], F32, name="back", tag="bank")
-        for b in range(2):
-            nc.tensor.transpose(
-                back[:, b, :],
-                by_slot[:, 2 * b : 2 * b + 2, :].rearrange("p r g -> p (r g)"),
-                ident[:],
-            )
+        nc.vector.tensor_reduce(
+            by_slot[:, :, 0:HG], early[:].rearrange("p r (g h) -> p r g h", h=H), AXIS.X, ALU.add
+        )
         padded = keep.tile([P, 2, P + 8], F32, name="padded")
         nc.gpsimd.memset(padded[:, :, 0:8], 0.0)
-        nc.scalar.activation(padded[:, :, 8:], back[:], ACT.Copy, scale=102.4)
-        smooth = pscore.tile([P, PACK + 2, G], F32, name="smooth", tag="bank")
+        for b in range(2):
+            nc.vector.tensor_reduce(
+                by_slot[:, 2 * b : 2 * b + 2, HG:G],
+                late[b][:].rearrange("p r (g h) -> p r g h", h=H), AXIS.X, ALU.add,
+            )
+            back = psum.tile([P, P], F32, name="back", tag=f"bank{b}")
+            nc.tensor.transpose(
+                back[:], by_slot[:, 2 * b : 2 * b + 2, :].rearrange("p r g -> p (r g)"), ident[:]
+            )
+            nc.scalar.activation(padded[:, b, 8:], back[:], ACT.Copy, scale=102.4)
+        smooth = psum.tile([P, PACK + 2, G], F32, name="smooth", tag="bank2")
         steps = []
         for b in range(2):
             for k in range(PACK - 2 * b):

@@ -5,6 +5,7 @@ from concourse.masks import make_identity
 
 D, T, I, Q, G = 512, 2048, 512, 1024, 64
 FLOPS = 2 * D * I * Q
+VOTE_SCALE = 102.4
 
 F32 = mybir.dt.float32
 BF16 = mybir.dt.bfloat16
@@ -20,18 +21,20 @@ AXIS = mybir.AxisListType
 
 P = 128
 PACK = 4
+QUADRANT = 32
 ROWS = Q // G
 GROUPS = 2
-HG = G // GROUPS
-H = P // HG
-TILES = ROWS // H
-BLOCKS = PACK // H
-SPILL = H - 1
-CHUNKS = [[0,16,[["s",0,16]]],[16,32,[["s",16,22],["v",22,32]]],[32,48,[["s",32,48]]],[48,64,[["s",48,54],["g",54,64]]]]
-QUANT = {0: 1, 1: 1, 2: 2, 4: 4}
-BATCHES = [[0,1],[2,3],[4,5,6],[7]]
+GROUP_HEADS = G // GROUPS
+TILE_ROWS = P // GROUP_HEADS
+TILES = ROWS // TILE_ROWS
+LAST = GROUPS * TILES - 1
+CHUNK_HEADS = GROUP_HEADS // 2
+HALVES = ((0, 2), (2, 4))
+PAD = 8
+SCALAR_HEADS = 10
 SCORE_BANKS = 4
-SCALE_ENG = "ggggvvvv"
+QUANTISE_CALLS = {0: 1, 1: 1, 2: 2}
+RECIPROCAL_CALLS = ((0, 1), (2, 3), (4, 5, 6), (7,))
 
 
 def tile_attend_votes_pl_kernel(tc, query, keys_words, keys_scales, offs, out_0, out_1, out_2):
@@ -40,27 +43,29 @@ def tile_attend_votes_pl_kernel(tc, query, keys_words, keys_scales, offs, out_0,
         keep = ctx.enter_context(tc.tile_pool(name="keep", bufs=1))
         psum = ctx.enter_context(tc.psum_pool(name="psum", bufs=1))
 
-        offsets = keep.tile([P, I // 16], U16, name="offsets")
-        nc.sync.dma_start(offsets[:], offs)
         pool_words = keep.tile([P, T], U16, name="pool_words", align_bytes=64)
         nc.sync.dma_start(pool_words[:].bitcast(I32), keys_words[0].bitcast(I32))
+        offsets = keep.tile([P, I // 16], U16, name="offsets")
+        nc.sync.dma_start(offsets[:], offs)
         pool_scales = keep.tile([P, T], U8, name="pool_scales", align_bytes=64)
         nc.vector.memset(pool_scales[:].bitcast(I32), 0)
-        for quad in range(4):
+        for quad in range(P // QUADRANT):
             nc.sync.dma_start(
-                pool_scales[32 * quad : 32 * quad + 4, :].bitcast(I32),
-                keys_scales[0, 4 * quad : 4 * quad + 4, :].bitcast(I32),
+                pool_scales[QUADRANT * quad : QUADRANT * quad + PACK, :].bitcast(I32),
+                keys_scales[0, PACK * quad : PACK * (quad + 1), :].bitcast(I32),
             )
         query_rows = query.rearrange("(p d) q -> p d q", d=PACK)
-        raws = []
-        for c, (g0, g1, parts) in enumerate(CHUNKS):
-            raw = keep.tile([P, PACK, (g1 - g0) * ROWS], F32, name=f"raw{c}")
-            nc.sync.dma_start(raw[:], query_rows[:, :, g0 * ROWS : g1 * ROWS])
-            raws.append(raw)
+        chunks = []
+        for c in range(G // CHUNK_HEADS):
+            chunk = keep.tile([P, PACK, CHUNK_HEADS * ROWS], F32, name=f"chunk{c}")
+            nc.sync.dma_start(
+                chunk[:], query_rows[:, :, c * CHUNK_HEADS * ROWS : (c + 1) * CHUNK_HEADS * ROWS]
+            )
+            chunks.append(chunk)
 
-        warm = keep.tile([P, 2], F32, name="warm")
-        nc.vector.memset(warm[:, 0:1], 0.0)
-        nc.scalar.activation(warm[:, 1:2], warm[:, 0:1], ACT.Exp)
+        preload = keep.tile([P, 2], F32, name="preload")
+        nc.vector.memset(preload[:, 0:1], 0.0)
+        nc.scalar.activation(preload[:, 1:2], preload[:, 0:1], ACT.Exp)
 
         ident = keep.tile([P, P], F32, name="ident")
         make_identity(nc, ident[:])
@@ -70,45 +75,67 @@ def tile_attend_votes_pl_kernel(tc, query, keys_words, keys_scales, offs, out_0,
         nc.vector.tensor_copy(key_words[:], pool_words[:].indirect(offsets[:]))
         nc.vector.tensor_copy(key_scales[:], pool_scales[:].indirect(offsets[:]))
 
-        grouped = [
-            keep.tile([P, TILES, HG, H, PACK], BF16, name=f"grouped{a}", align_bytes=64)
+        rounded = [
+            keep.tile([P, TILES, GROUP_HEADS, TILE_ROWS, PACK], BF16, name=f"rounded{a}", align_bytes=64)
             for a in range(GROUPS)
         ]
-        for c, (g0, g1, parts) in enumerate(CHUNKS):
-            for eng, e0, e1 in parts:
-                a = e0 // HG
-                src = raws[c][:, :, (e0 - g0) * ROWS : (e1 - g0) * ROWS]
-                dst = grouped[a][:, :, e0 - a * HG : e1 - a * HG, :, :]
-                if eng == "g":
-                    nc.gpsimd.tensor_scalar(
-                        dst.rearrange("p t g h d -> p g t h d"),
-                        src.rearrange("p d (g t h) -> p g t h d", t=TILES, h=H),
-                        1.0, 0.0, ALU.mult, ALU.add,
-                    )
-                else:
-                    copy = nc.vector.tensor_copy if eng == "v" else nc.scalar.copy
-                    copy(
-                        dst.rearrange("p t g h d -> p g t h d"),
-                        src.rearrange("p d (g t h) -> p g t h d", t=TILES, h=H),
-                    )
+
+        def gpsimd_copy(dst, src):
+            nc.gpsimd.tensor_scalar(dst, src, 1.0, 0.0, ALU.mult, ALU.add)
+
+        def round_queries(copy, c, heads, tiles):
+            src = chunks[c][:, :, heads.start * ROWS : heads.stop * ROWS].rearrange(
+                "p d (g t h) -> p g t h d", t=TILES, h=TILE_ROWS
+            )
+            first = (c % 2) * CHUNK_HEADS
+            dst = rounded[c // 2][:, tiles, first + heads.start : first + heads.stop, :, :]
+            copy(dst.rearrange("p t g h d -> p g t h d"), src[:, :, tiles, :, :])
+
+        all_heads, all_tiles = slice(0, CHUNK_HEADS), slice(0, TILES)
+        round_queries(nc.scalar.copy, 0, all_heads, all_tiles)
+        round_queries(nc.vector.tensor_copy, 1, all_heads, slice(0, 1))
+        round_queries(nc.scalar.copy, 1, all_heads, slice(1, 3))
+        round_queries(nc.vector.tensor_copy, 1, all_heads, slice(3, 4))
+        round_queries(nc.scalar.copy, 2, slice(0, SCALAR_HEADS), all_tiles)
+        round_queries(nc.vector.tensor_copy, 2, slice(SCALAR_HEADS, CHUNK_HEADS), all_tiles)
+        round_queries(nc.vector.tensor_copy, 3, all_heads, slice(0, 1))
+        round_queries(nc.scalar.copy, 3, all_heads, slice(1, 2))
+        round_queries(gpsimd_copy, 3, all_heads, slice(2, 4))
 
         y = keep.tile([P, PACK, G], F32, name="y")
         y_bf = keep.tile([P, G, PACK], BF16, name="y_bf", align_bytes=64)
-
         q_codes = [keep.tile([P, TILES * P], U32, name=f"q_codes{a}", align_bytes=64) for a in range(GROUPS)]
         q_scales = [keep.tile([P, TILES * P], U8, name=f"q_scales{a}", align_bytes=64) for a in range(GROUPS)]
-        early = psum.tile([P, PACK, P], F32, name="early")
-        late = [psum.tile([P, 2, P], F32, name=f"late{b}") for b in range(2)]
-        probs = []
-        for a in range(GROUPS):
-            for t in range(TILES):
-                n = a * TILES + t
-                if n in QUANT:
-                    cols = slice(t * P, (t + QUANT[n]) * P)
+
+        first_sums = psum.tile([P, PACK, P], F32, name="first_sums")
+        second_sums = [psum.tile([P, 2, P], F32, name=f"second_sums{b}") for b in range(len(HALVES))]
+
+        def add_turned(n, weights, r):
+            if n < TILES:
+                target, places = first_sums[:, r, :], PACK
+            else:
+                target, places = second_sums[r // 2][:, r % 2, :], 2
+            nc.tensor.matmul(
+                target,
+                lhsT=weights[:, r, :],
+                rhs=ident[:],
+                start=(n % TILES == 0 and r % places == 0),
+                stop=(n % TILES == TILES - 1 and r % places == places - 1),
+                is_transpose=True,
+            )
+
+        probs, weights = [], []
+        for batch in RECIPROCAL_CALLS:
+            row_sums = keep.tile([P, len(batch)], F32, name=f"row_sums{batch[0]}")
+            for place, n in enumerate(batch):
+                a, t = divmod(n, TILES)
+                if t in QUANTISE_CALLS:
+                    served = slice(t, t + QUANTISE_CALLS[t])
+                    served_cols = slice(served.start * P, served.stop * P)
                     nc.vector.quantize_mx(
-                        out=q_codes[a][:, cols].bitcast(FP8X4),
-                        scales=q_scales[a][:, cols],
-                        in_=grouped[a][:, t : t + QUANT[n], :, :, :].rearrange("p t g h d -> p (t g h d)"),
+                        out=q_codes[a][:, served_cols].bitcast(FP8X4),
+                        scales=q_scales[a][:, served_cols],
+                        in_=rounded[a][:, served, :, :, :].rearrange("p t g h d -> p (t g h d)"),
                     )
                 cols = slice(t * P, (t + 1) * P)
                 scores = psum.tile([P, I], F32, name="scores", tag=f"bank{n % SCORE_BANKS}")
@@ -123,84 +150,103 @@ def tile_attend_votes_pl_kernel(tc, query, keys_words, keys_scales, offs, out_0,
                 )
                 neg_max = keep.tile([P, 1], F32, name=f"neg_max{n}")
                 nc.vector.tensor_reduce(neg_max[:], scores[:], AXIS.X, ALU.max, negate=True)
-                probs.append(keep.tile([P, PACK, P], F32, name=f"probs{n}"))
-                batch = [bt for bt in BATCHES if n in bt][0]
-                if n == batch[0]:
-                    row_sum = keep.tile([P, len(batch)], F32, name=f"row_sum{n}")
-                place = n - batch[0]
+                probs.append(keep.tile([P, PACK, P], F32, name="probs", tag=f"probs{n}"))
                 nc.scalar.activation(
-                    probs[n][:], scores[:].rearrange("p (s r) -> p r s", r=PACK), ACT.Exp,
-                    bias=neg_max[:], accum_out=row_sum[:, place : place + 1],
+                    probs[n][:],
+                    scores[:].rearrange("p (s r) -> p r s", r=PACK),
+                    ACT.Exp,
+                    bias=neg_max[:],
+                    accum_out=row_sums[:, place : place + 1],
                 )
-                if n != batch[-1]:
-                    continue
-                inv_sum = keep.tile([P, len(batch)], F32, name=f"inv_sum{n}")
-                nc.vector.reciprocal(inv_sum[:], row_sum[:])
-                for m in batch:
-                    inv = inv_sum[:, m - batch[0] : m - batch[0] + 1]
-                    weights = keep.tile([P, PACK, P], F32, name=f"weights{m}")
-                    if SCALE_ENG[m] == "s":
-                        nc.scalar.activation(weights[:], probs[m][:], ACT.Copy, scale=inv)
-                    elif SCALE_ENG[m] == "v":
-                        cuts = (0, 2, 4) if m == GROUPS * TILES - 1 else (0, 4)
-                        for r0, r1 in zip(cuts, cuts[1:]):
-                            nc.vector.tensor_scalar(weights[:, r0:r1, :], probs[m][:, r0:r1, :], inv, None, ALU.mult)
+            inv_sums = keep.tile([P, len(batch)], F32, name=f"inv_sums{batch[0]}")
+            nc.vector.reciprocal(inv_sums[:], row_sums[:])
+            for place, n in enumerate(batch):
+                inv = inv_sums[:, place : place + 1]
+                weights.append(keep.tile([P, PACK, P], F32, name=f"weights{n}"))
+                if n == LAST - 1:
+                    for r0, r1 in HALVES:
+                        nc.scalar.activation(weights[n][:, r0:r1, :], probs[n][:, r0:r1, :], ACT.Copy, scale=inv)
+                elif n == LAST:
+                    for r0, r1 in HALVES:
+                        nc.vector.tensor_scalar(weights[n][:, r0:r1, :], probs[n][:, r0:r1, :], inv, None, ALU.mult)
+                        for m in (LAST - 1, LAST):
+                            for r in range(r0, r1):
+                                add_turned(m, weights[m], r)
+                else:
+                    if n < TILES:
+                        nc.gpsimd.tensor_scalar(weights[n][:], probs[n][:], inv, 0.0, ALU.mult, ALU.add)
                     else:
-                        nc.gpsimd.tensor_scalar(weights[:], probs[m][:], inv, 0.0, ALU.mult, ALU.add)
-                    span = PACK if a == 0 else 2
+                        nc.vector.tensor_scalar(weights[n][:], probs[n][:], inv, None, ALU.mult)
                     for r in range(PACK):
-                        nc.tensor.matmul(
-                            early[:, r, :] if a == 0 else late[r // 2][:, r % 2, :], lhsT=weights[:, r, :], rhs=ident[:],
-                            start=(m % TILES == 0 and r % span == 0), stop=(m % TILES == TILES - 1 and r % span == span - 1),
-                            is_transpose=True,
-                        )
+                        add_turned(n, weights[n], r)
 
-        by_slot = keep.tile([P, PACK, G], F32, name="by_slot")
+        votes = keep.tile([P, PACK, G], F32, name="votes", tag=f"probs{LAST}")
         nc.vector.tensor_reduce(
-            by_slot[:, :, 0:HG], early[:].rearrange("p r (g h) -> p r g h", h=H), AXIS.X, ALU.add
+            votes[:, :, 0:GROUP_HEADS],
+            first_sums[:].rearrange("p r (g h) -> p r g h", h=TILE_ROWS),
+            AXIS.X,
+            ALU.add,
         )
-        padded = keep.tile([P, 2, P + 8], F32, name="padded")
-        nc.gpsimd.memset(padded[:, :, 0:8], 0.0)
-        for b in range(2):
+
+        zeros = keep.tile([P, P], F32, name="zeros")
+        nc.gpsimd.memset(zeros[:], 0.0)
+        turned = [psum.tile([P, PAD + P], F32, name="turned", tag=f"bank{b}") for b in range(len(HALVES))]
+        nc.tensor.transpose(turned[1][:, 0:P], zeros[:], ident[:])
+        low = keep.tile([P, PAD + P], F32, name="low")
+        both = keep.tile([P, PAD + P], F32, name="both")
+        high = keep.tile([P, P], F32, name="high")
+        across = keep.tile([P, P], F32, name="across")
+        nc.gpsimd.memset(low[:, 0:PAD], 0.0)
+        nc.gpsimd.memset(both[:, 0:PAD], 0.0)
+        for b, (r0, r1) in enumerate(HALVES):
             nc.vector.tensor_reduce(
-                by_slot[:, 2 * b : 2 * b + 2, HG:G],
-                late[b][:].rearrange("p r (g h) -> p r g h", h=H), AXIS.X, ALU.add,
+                votes[:, r0:r1, GROUP_HEADS:G],
+                second_sums[b][:].rearrange("p r (g h) -> p r g h", h=TILE_ROWS),
+                AXIS.X,
+                ALU.add,
             )
-            back = psum.tile([P, P], F32, name="back", tag=f"bank{b}")
-            nc.tensor.transpose(
-                back[:], by_slot[:, 2 * b : 2 * b + 2, :].rearrange("p r g -> p (r g)"), ident[:]
-            )
-            nc.scalar.activation(padded[:, b, 8:], back[:], ACT.Copy, scale=102.4)
-        smooth = psum.tile([P, PACK + 2, G], F32, name="smooth", tag="bank2")
-        steps = []
-        for b in range(2):
-            for k in range(PACK - 2 * b):
-                steps.append((b, 8, 2 * b + k))
-            for k in range(2 * b + 2):
-                steps.append((b, 7, 2 * b - k))
-        lead = [[s for s in steps if s[2] == j][0] for j in (-1, 1, 3)]
-        steps = lead + [s for s in steps if s not in lead]
-        for m, (b, c0, j) in enumerate(steps):
+            nc.tensor.transpose(turned[b][:, PAD:], votes[:, r0:r1, :].rearrange("p r g -> p (r g)"), ident[:])
+        at_s, before_s = slice(PAD, PAD + P), slice(PAD - 1, PAD - 1 + P)
+        nc.scalar.activation(low[:, at_s], turned[0][:, at_s], ACT.Copy, scale=VOTE_SCALE)
+        nc.vector.scalar_tensor_tensor(across[:], turned[1][:, before_s], VOTE_SCALE, low[:, at_s], ALU.mult, ALU.add)
+        nc.vector.scalar_tensor_tensor(both[:, at_s], turned[1][:, at_s], VOTE_SCALE, low[:, at_s], ALU.mult, ALU.add)
+        nc.scalar.activation(high[:], turned[1][:, at_s], ACT.Copy, scale=VOTE_SCALE)
+
+        smooth = psum.tile([P, PACK + 2, G], F32, name="smooth")
+        terms = (
+            (across[:], 1),
+            (both[:, before_s], -1),
+            (both[:, at_s], 3),
+            (across[:], 0),
+            (across[:], 2),
+            (low[:, before_s], 0),
+            (high[:], 2),
+        )
+        for m, (source, j) in enumerate(terms):
             nc.tensor.matmul(
                 smooth[:, 1 + j : 3 + j, :].rearrange("p j g -> p (j g)"),
-                lhsT=padded[:, b, c0 : c0 + P], rhs=ident[:],
-                start=(m == 0), stop=(m == len(steps) - 1), is_transpose=True,
+                lhsT=source,
+                rhs=ident[:],
+                start=(m == 0),
+                stop=(m == len(terms) - 1),
+                is_transpose=True,
             )
+
         result = smooth[:, 1 : 1 + PACK, :]
         nc.vector.tensor_copy(y_bf[:], result.rearrange("p r g -> p g r"))
         nc.scalar.copy(y[:], result)
-
         y_codes = keep.tile([P, G], U32, name="y_codes", align_bytes=64)
         y_scales = keep.tile([P, G], U8, name="y_scales", align_bytes=64)
         nc.vector.quantize_mx(
-            out=y_codes[:].bitcast(FP8X4), scales=y_scales[:],
+            out=y_codes[:].bitcast(FP8X4),
+            scales=y_scales[:],
             in_=y_bf[:].rearrange("p g r -> p (g r)"),
         )
+
         nc.sync.dma_start(out_1[0].rearrange("p c r -> p (c r)").bitcast(I32), y_codes[:].bitcast(I32))
         nc.scalar.dma_start(out_0.rearrange("(s r) g -> s r g", r=PACK), y[:])
-        for quad in range(4):
-            queue = nc.sync if quad < 2 else nc.scalar
+        for quad, queue in enumerate((nc.sync, nc.sync, nc.scalar, nc.scalar)):
             queue.dma_start(
-                out_2[0, 4 * quad : 4 * quad + 4, :].bitcast(I32),
-                y_scales[32 * quad : 32 * quad + 4, :].bitcast(I32),
+                out_2[0, PACK * quad : PACK * (quad + 1), :].bitcast(I32),
+                y_scales[QUADRANT * quad : QUADRANT * quad + PACK, :].bitcast(I32),
             )

from contextlib import ExitStack

import concourse.mybir as mybir
from concourse.masks import make_identity

D, T, I, Q, G = 512, 2048, 512, 1024, 64
FLOPS = 2 * D * I * Q
VOTE_SCALE = 102.4

F32 = mybir.dt.float32
BF16 = mybir.dt.bfloat16
I32 = mybir.dt.int32
U32 = mybir.dt.uint32
U16 = mybir.dt.uint16
U8 = mybir.dt.uint8
FP8X4 = mybir.dt.float8_e4m3fn_x4
FP4X4 = mybir.dt.float4_e2m1fn_x4
ALU = mybir.AluOpType
ACT = mybir.ActivationFunctionType
AXIS = mybir.AxisListType

P = 128
PACK = 4
QUADRANT = 32
ROWS = Q // G
GROUPS = 2
GROUP_HEADS = G // GROUPS
TILE_ROWS = P // GROUP_HEADS
TILES = ROWS // TILE_ROWS
LAST = GROUPS * TILES - 1
CHUNK_HEADS = GROUP_HEADS // 2
HALVES = ((0, 2), (2, 4))
PAD = 8
SCALAR_HEADS = 10
SCORE_BANKS = 4
QUANTISE_CALLS = {0: 1, 1: 1, 2: 2}
RECIPROCAL_CALLS = ((0, 1), (2, 3), (4, 5, 6), (7,))


def tile_attend_votes_pl_kernel(tc, query, keys_words, keys_scales, offs, out_0, out_1, out_2):
    nc = tc.nc
    with ExitStack() as ctx:
        keep = ctx.enter_context(tc.tile_pool(name="keep", bufs=1))
        psum = ctx.enter_context(tc.psum_pool(name="psum", bufs=1))

        pool_words = keep.tile([P, T], U16, name="pool_words", align_bytes=64)
        nc.sync.dma_start(pool_words[:].bitcast(I32), keys_words[0].bitcast(I32))
        offsets = keep.tile([P, I // 16], U16, name="offsets")
        nc.sync.dma_start(offsets[:], offs)
        pool_scales = keep.tile([P, T], U8, name="pool_scales", align_bytes=64)
        nc.vector.memset(pool_scales[:].bitcast(I32), 0)
        for quad in range(P // QUADRANT):
            nc.sync.dma_start(
                pool_scales[QUADRANT * quad : QUADRANT * quad + PACK, :].bitcast(I32),
                keys_scales[0, PACK * quad : PACK * (quad + 1), :].bitcast(I32),
            )
        query_rows = query.rearrange("(p d) q -> p d q", d=PACK)
        chunks = []
        for c in range(G // CHUNK_HEADS):
            chunk = keep.tile([P, PACK, CHUNK_HEADS * ROWS], F32, name=f"chunk{c}")
            nc.sync.dma_start(
                chunk[:], query_rows[:, :, c * CHUNK_HEADS * ROWS : (c + 1) * CHUNK_HEADS * ROWS]
            )
            chunks.append(chunk)

        preload = keep.tile([P, 2], F32, name="preload")
        nc.vector.memset(preload[:, 0:1], 0.0)
        nc.scalar.activation(preload[:, 1:2], preload[:, 0:1], ACT.Exp)

        ident = keep.tile([P, P], F32, name="ident")
        make_identity(nc, ident[:])

        key_words = keep.tile([P, I], U16, name="key_words", align_bytes=64)
        key_scales = keep.tile([P, I], U8, name="key_scales", align_bytes=64)
        nc.vector.tensor_copy(key_words[:], pool_words[:].indirect(offsets[:]))
        nc.vector.tensor_copy(key_scales[:], pool_scales[:].indirect(offsets[:]))

        rounded = [
            keep.tile([P, TILES, GROUP_HEADS, TILE_ROWS, PACK], BF16, name=f"rounded{a}", align_bytes=64)
            for a in range(GROUPS)
        ]

        def gpsimd_copy(dst, src):
            nc.gpsimd.tensor_scalar(dst, src, 1.0, 0.0, ALU.mult, ALU.add)

        def round_queries(copy, c, heads, tiles):
            src = chunks[c][:, :, heads.start * ROWS : heads.stop * ROWS].rearrange(
                "p d (g t h) -> p g t h d", t=TILES, h=TILE_ROWS
            )
            first = (c % 2) * CHUNK_HEADS
            dst = rounded[c // 2][:, tiles, first + heads.start : first + heads.stop, :, :]
            copy(dst.rearrange("p t g h d -> p g t h d"), src[:, :, tiles, :, :])

        all_heads, all_tiles = slice(0, CHUNK_HEADS), slice(0, TILES)
        round_queries(nc.scalar.copy, 0, all_heads, all_tiles)
        round_queries(nc.vector.tensor_copy, 1, all_heads, slice(0, 1))
        round_queries(nc.scalar.copy, 1, all_heads, slice(1, 3))
        round_queries(nc.vector.tensor_copy, 1, all_heads, slice(3, 4))
        round_queries(nc.scalar.copy, 2, slice(0, SCALAR_HEADS), all_tiles)
        round_queries(nc.vector.tensor_copy, 2, slice(SCALAR_HEADS, CHUNK_HEADS), all_tiles)
        round_queries(nc.vector.tensor_copy, 3, all_heads, slice(0, 1))
        round_queries(nc.scalar.copy, 3, all_heads, slice(1, 2))
        round_queries(gpsimd_copy, 3, all_heads, slice(2, 4))

        y = keep.tile([P, PACK, G], F32, name="y")
        y_bf = keep.tile([P, G, PACK], BF16, name="y_bf", align_bytes=64)
        q_codes = [keep.tile([P, TILES * P], U32, name=f"q_codes{a}", align_bytes=64) for a in range(GROUPS)]
        q_scales = [keep.tile([P, TILES * P], U8, name=f"q_scales{a}", align_bytes=64) for a in range(GROUPS)]

        first_sums = psum.tile([P, PACK, P], F32, name="first_sums")
        second_sums = [psum.tile([P, 2, P], F32, name=f"second_sums{b}") for b in range(len(HALVES))]

        def add_turned(n, weights, r):
            if n < TILES:
                target, places = first_sums[:, r, :], PACK
            else:
                target, places = second_sums[r // 2][:, r % 2, :], 2
            nc.tensor.matmul(
                target,
                lhsT=weights[:, r, :],
                rhs=ident[:],
                start=(n % TILES == 0 and r % places == 0),
                stop=(n % TILES == TILES - 1 and r % places == places - 1),
                is_transpose=True,
            )

        probs, weights = [], []
        for batch in RECIPROCAL_CALLS:
            row_sums = keep.tile([P, len(batch)], F32, name=f"row_sums{batch[0]}")
            for place, n in enumerate(batch):
                a, t = divmod(n, TILES)
                if t in QUANTISE_CALLS:
                    served = slice(t, t + QUANTISE_CALLS[t])
                    served_cols = slice(served.start * P, served.stop * P)
                    nc.vector.quantize_mx(
                        out=q_codes[a][:, served_cols].bitcast(FP8X4),
                        scales=q_scales[a][:, served_cols],
                        in_=rounded[a][:, served, :, :, :].rearrange("p t g h d -> p (t g h d)"),
                    )
                cols = slice(t * P, (t + 1) * P)
                scores = psum.tile([P, I], F32, name="scores", tag=f"bank{n % SCORE_BANKS}")
                nc.tensor.matmul_mx(
                    out=scores[:],
                    lhsT=q_codes[a][:, cols].bitcast(FP8X4),
                    lhsT_scale=q_scales[a][:, cols],
                    rhs=key_words[:].bitcast(FP4X4),
                    rhs_scale=key_scales[:],
                    start=True,
                    stop=True,
                )
                neg_max = keep.tile([P, 1], F32, name=f"neg_max{n}")
                nc.vector.tensor_reduce(neg_max[:], scores[:], AXIS.X, ALU.max, negate=True)
                probs.append(keep.tile([P, PACK, P], F32, name="probs", tag=f"probs{n}"))
                nc.scalar.activation(
                    probs[n][:],
                    scores[:].rearrange("p (s r) -> p r s", r=PACK),
                    ACT.Exp,
                    bias=neg_max[:],
                    accum_out=row_sums[:, place : place + 1],
                )
            inv_sums = keep.tile([P, len(batch)], F32, name=f"inv_sums{batch[0]}")
            nc.vector.reciprocal(inv_sums[:], row_sums[:])
            for place, n in enumerate(batch):
                inv = inv_sums[:, place : place + 1]
                weights.append(keep.tile([P, PACK, P], F32, name=f"weights{n}"))
                if n == LAST - 1:
                    for r0, r1 in HALVES:
                        nc.scalar.activation(weights[n][:, r0:r1, :], probs[n][:, r0:r1, :], ACT.Copy, scale=inv)
                elif n == LAST:
                    for r0, r1 in HALVES:
                        nc.vector.tensor_scalar(weights[n][:, r0:r1, :], probs[n][:, r0:r1, :], inv, None, ALU.mult)
                        for m in (LAST - 1, LAST):
                            for r in range(r0, r1):
                                add_turned(m, weights[m], r)
                else:
                    if n < TILES:
                        nc.gpsimd.tensor_scalar(weights[n][:], probs[n][:], inv, 0.0, ALU.mult, ALU.add)
                    else:
                        nc.vector.tensor_scalar(weights[n][:], probs[n][:], inv, None, ALU.mult)
                    for r in range(PACK):
                        add_turned(n, weights[n], r)

        votes = keep.tile([P, PACK, G], F32, name="votes", tag=f"probs{LAST}")
        nc.vector.tensor_reduce(
            votes[:, :, 0:GROUP_HEADS],
            first_sums[:].rearrange("p r (g h) -> p r g h", h=TILE_ROWS),
            AXIS.X,
            ALU.add,
        )

        zeros = keep.tile([P, P], F32, name="zeros")
        nc.gpsimd.memset(zeros[:], 0.0)
        turned = [psum.tile([P, PAD + P], F32, name="turned", tag=f"bank{b}") for b in range(len(HALVES))]
        nc.tensor.transpose(turned[1][:, 0:P], zeros[:], ident[:])
        low = keep.tile([P, PAD + P], F32, name="low")
        both = keep.tile([P, PAD + P], F32, name="both")
        high = keep.tile([P, P], F32, name="high")
        across = keep.tile([P, P], F32, name="across")
        nc.gpsimd.memset(low[:, 0:PAD], 0.0)
        nc.gpsimd.memset(both[:, 0:PAD], 0.0)
        for b, (r0, r1) in enumerate(HALVES):
            nc.vector.tensor_reduce(
                votes[:, r0:r1, GROUP_HEADS:G],
                second_sums[b][:].rearrange("p r (g h) -> p r g h", h=TILE_ROWS),
                AXIS.X,
                ALU.add,
            )
            nc.tensor.transpose(turned[b][:, PAD:], votes[:, r0:r1, :].rearrange("p r g -> p (r g)"), ident[:])
        at_s, before_s = slice(PAD, PAD + P), slice(PAD - 1, PAD - 1 + P)
        nc.scalar.activation(low[:, at_s], turned[0][:, at_s], ACT.Copy, scale=VOTE_SCALE)
        nc.vector.scalar_tensor_tensor(across[:], turned[1][:, before_s], VOTE_SCALE, low[:, at_s], ALU.mult, ALU.add)
        nc.vector.scalar_tensor_tensor(both[:, at_s], turned[1][:, at_s], VOTE_SCALE, low[:, at_s], ALU.mult, ALU.add)
        nc.scalar.activation(high[:], turned[1][:, at_s], ACT.Copy, scale=VOTE_SCALE)

        smooth = psum.tile([P, PACK + 2, G], F32, name="smooth")
        terms = (
            (across[:], 1),
            (both[:, before_s], -1),
            (both[:, at_s], 3),
            (across[:], 0),
            (across[:], 2),
            (low[:, before_s], 0),
            (high[:], 2),
        )
        for m, (source, j) in enumerate(terms):
            nc.tensor.matmul(
                smooth[:, 1 + j : 3 + j, :].rearrange("p j g -> p (j g)"),
                lhsT=source,
                rhs=ident[:],
                start=(m == 0),
                stop=(m == len(terms) - 1),
                is_transpose=True,
            )

        result = smooth[:, 1 : 1 + PACK, :]
        nc.vector.tensor_copy(y_bf[:], result.rearrange("p r g -> p g r"))
        nc.scalar.copy(y[:], result)
        y_codes = keep.tile([P, G], U32, name="y_codes", align_bytes=64)
        y_scales = keep.tile([P, G], U8, name="y_scales", align_bytes=64)
        nc.vector.quantize_mx(
            out=y_codes[:].bitcast(FP8X4),
            scales=y_scales[:],
            in_=y_bf[:].rearrange("p g r -> p (g r)"),
        )

        nc.sync.dma_start(out_1[0].rearrange("p c r -> p (c r)").bitcast(I32), y_codes[:].bitcast(I32))
        nc.scalar.dma_start(out_0.rearrange("(s r) g -> s r g", r=PACK), y[:])
        for quad, queue in enumerate((nc.sync, nc.sync, nc.scalar, nc.scalar)):
            queue.dma_start(
                out_2[0, PACK * quad : PACK * (quad + 1), :].bitcast(I32),
                y_scales[QUADRANT * quad : QUADRANT * quad + PACK, :].bitcast(I32),
            )
